import numpy as np
import ml_dtypes


def mxq(x, axis, fmt="e4m3"):
    dtype, down = {"e4m3": (ml_dtypes.float8_e4m3fn, 7), "e5m2": (ml_dtypes.float8_e5m2, 14)}[fmt]
    v = np.moveaxis(np.asarray(x, np.float32).astype(ml_dtypes.bfloat16).astype(np.float64), axis, -1)
    blocks = v.reshape(v.shape[:-1] + (-1, 32))
    amax = np.abs(blocks).max(-1, keepdims=True)
    byte = np.maximum(np.where(amax > 0, np.frexp(amax)[1] - 1 + 127, 0) - down, 1)
    scale = np.exp2(byte - 127.0)
    codes = (blocks / scale).astype(np.float32).astype(dtype).astype(np.float64)
    return np.moveaxis((codes * scale).reshape(v.shape), -1, axis)


WIDE = False


def mx_kscale(k):
    if not WIDE:
        return np.ones(k)
    levels = np.array([10, -10, 5, -5, 0])
    if k % 512:
        return np.exp2(np.random.permutation(np.resize(levels, k // 32))).repeat(32)
    a = np.empty((k // 512, 16))
    for p in range(k // 512):
        a[p, :8] = np.random.permutation(np.resize(levels, 8))
        for g in range(8):
            far = levels[np.abs(levels - a[p, g]) >= 10]
            a[p, g + 8] = far[np.random.randint(len(far))]
    return np.exp2(a.ravel()).repeat(32)


def f64(x):
    return np.asarray(x).astype(np.float64)


def striped(idx):
    return np.tile(idx.reshape(-1, 16).T, (8, 1)).astype(np.uint16)


def unstriped(offs):
    return offs[:16].T.reshape(-1).astype(np.int64)


def gelu(v):
    return 0.5 * v * (1.0 + np.tanh(np.sqrt(2.0 / np.pi) * (v + 0.044715 * v**3)))


K, T, E, C, H, N = 1024, 2048, 2, 256, 512, 512


def by_expert(wq, xq):
    return np.concatenate([wq[e].T @ xq[:, e * C:(e + 1) * C] for e in range(E)], axis=1)


def setup_inputs():
    n = np.random.standard_normal
    s = mx_kscale(K)[:, None]
    u = mx_kscale(H)
    return {
        "xT": (n((K, T)) * s).astype(np.float32),
        "w1": (n((E, K, H)) / np.sqrt(K) / s[None]).astype(np.float32),
        "w3": (n((E, K, H)) / np.sqrt(K) / s[None] * u[None, None, :]).astype(np.float32),
        "w2": (n((E, H, N)) / np.sqrt(H) / u[None, :, None]).astype(np.float32),
        "gate": np.tile(np.random.uniform(0.2, 1.0, E * C), (N, 1)).astype(np.float32),
        "offs": striped(np.random.permutation(T)[:E * C]),
    }


def reference(xT, w1, w3, w2, gate, offs):
    idx = unstriped(offs)
    xq = mxq(f64(xT)[:, idx], 0, "e4m3")
    h = gelu(by_expert(mxq(f64(w1), 1, "e4m3"), xq))
    h = h * by_expert(mxq(f64(w3), 1, "e4m3"), xq)
    y = by_expert(mxq(f64(w2), 1, "e4m3"), mxq(h, 0, "e4m3"))
    out = np.zeros((N, T))
    out[:, idx] = f64(gate) * y
    return out

@@ -1,0 +1,239 @@
+from contextlib import ExitStack
+
+import concourse.mybir as mybir
+
+K, T, E, C, H, N = 1024, 2048, 2, 256, 512, 512
+SLOTS = E * C
+FLOPS = 2 * SLOTS * (2 * K * H + H * N)
+
+F32 = mybir.dt.float32
+BF16 = mybir.dt.bfloat16
+U32 = mybir.dt.uint32
+U16 = mybir.dt.uint16
+U8 = mybir.dt.uint8
+FP8X4 = mybir.dt.float8_e4m3fn_x4
+GELU = mybir.ActivationFunctionType.Gelu_apprx_tanh
+MULT = mybir.AluOpType.mult
+
+P = 128
+PACK = 4
+PASSES = K // (P * PACK)
+CHUNK = 128
+CHUNKS = C // CHUNK
+BLOCKS = N // P
+PAIRS = BLOCKS // 2
+LIST_COLS = C // 16
+LINE = 4
+TABLE_COLS = 8
+
+LOADS = (
+    tuple(("x", g, t) for g in range(PASSES) for t in range(PACK))
+    + tuple((mat, 0, g) for mat in ("w3", "w1") for g in range(PASSES))
+    + (("w3", 1, 0), ("w3", 1, 1), ("w1", 1, 0), ("w2", 0, 0), ("w1", 1, 1))
+    + (("gate", 0, 0), ("w2", 1, 0), ("gate", 1, 0), ("gate", 0, 1), ("gate", 1, 1))
+)
+LOADS_AHEAD = 4
+LOAD_BUFFERS = 6
+GROUPED_BUFFERS = 4
+Y_BUFFERS = 3
+
+VECTOR_GROUPS = {("w3", 0): 64, ("w1", 0): 64, ("w3", 1): 64, ("w1", 1): 64, ("w2", 0): 48, ("w2", 1): 0}
+
+SCATTER_TURNS = ((0, 1), (0, 1), (0, 1), (1, 0))
+
+
+def tile_routed_moe_kernel(tc, xT, w1, w3, w2, gate, offs, out):
+    nc = tc.nc
+    with ExitStack() as ctx:
+        held = ctx.enter_context(tc.tile_pool(name="held", bufs=1))
+        ring = ctx.enter_context(tc.tile_pool(name="ring", bufs=LOAD_BUFFERS))
+        work = ctx.enter_context(tc.tile_pool(name="work", bufs=E))
+        psum = ctx.enter_context(tc.psum_pool(name="psum", bufs=2))
+
+        offsets = held.tile([P, SLOTS // 16], U16, name="offsets")
+        nc.sync.dma_start(offsets[:], offs)
+
+        table_in = held.tile([P, TABLE_COLS], F32, name="table_in")
+        table_out = held.tile([P, TABLE_COLS], F32, name="table_out")
+        nc.vector.memset(table_in[:], 0.0)
+        nc.scalar.activation(out=table_out[:], in_=table_in[:], func=GELU)
+
+        windows = [held.tile([P, T], F32, name="window%d" % b) for b in range(BLOCKS)]
+        for b in range(BLOCKS):
+            nc.gpsimd.memset(windows[b][:], 0.0)
+
+        picked = [held.tile([P, PACK, SLOTS], F32, name="picked%d" % g) for g in range(PASSES)]
+        x_grouped = held.tile([P, PASSES, SLOTS, PACK], BF16, name="x_grouped", align_bytes=64)
+        x_codes = held.tile([P, PASSES, SLOTS], U32, name="x_codes", align_bytes=64)
+        x_scales = held.tile([P, PASSES, SLOTS], U8, name="x_scales", align_bytes=64)
+        w_codes = {}
+        w_scales = {}
+        for e in range(E):
+            for mat, passes in (("w1", PASSES), ("w3", PASSES), ("w2", 1)):
+                w_codes[(mat, e)] = held.tile([P, passes, H], U32, name="%s_codes%d" % (mat, e), align_bytes=64)
+                w_scales[(mat, e)] = held.tile([P, passes, H], U8, name="%s_scales%d" % (mat, e), align_bytes=64)
+        h_codes = [held.tile([P, C], U32, name="h_codes%d" % e, align_bytes=64) for e in range(E)]
+        h_scales = [held.tile([P, C], U8, name="h_scales%d" % e, align_bytes=64) for e in range(E)]
+        gate_sb = {}
+        for e in range(E):
+            for pair in range(PAIRS):
+                gate_sb[(e, pair)] = held.tile([P, 2, C], F32, name="gate_sb%d%d" % (e, pair))
+
+        x_planes = xT.rearrange("(g p t) v -> g p t v", p=P, t=PACK)
+        w_passes = {
+            "w1": w1.rearrange("e (g p t) i -> e g p t i", p=P, t=PACK),
+            "w3": w3.rearrange("e (g p t) i -> e g p t i", p=P, t=PACK),
+            "w2": w2.rearrange("e (g p u) n -> e g p u n", p=P, u=PACK),
+        }
+        gate_blocks = gate.rearrange("(b p) j -> p b j", p=P)
+
+        landed = {}
+        w3_banks = {}
+        gelu_tiles = {}
+        y_tiles = {}
+        turn = [0] * BLOCKS
+        written = set()
+
+        def load(item):
+            if item[0] == "gate":
+                e, pair = item[1:]
+                nc.sync.dma_start(gate_sb[(e, pair)][:], gate_blocks[:, 2 * pair:2 * pair + 2, e * C:(e + 1) * C])
+            elif item[0] == "x":
+                g, t = item[1:]
+                landed[item] = ring.tile([P, T], F32, name="plane", tag="landed")
+                nc.sync.dma_start(landed[item][:], x_planes[g, :, t, :])
+            else:
+                mat, e, g = item
+                landed[item] = ring.tile([P, PACK, H], F32, name="rows", tag="landed")
+                nc.sync.dma_start(landed[item][:], w_passes[mat][e, g])
+
+        def quantize(codes, scales, grouped):
+            nc.vector.quantize_mx(out=codes.bitcast(FP8X4), scales=scales, in_=grouped)
+
+        def gather_plane(g, t):
+            nc.vector.tensor_copy(picked[g][:, t, :], landed[("x", g, t)][:].indirect(offsets[:]))
+            nc.scalar.copy(out=x_grouped[:, g, :, t], in_=picked[g][:, t, :])
+            if (g, t) == (PASSES - 1, PACK - 1):
+                quantize(
+                    x_codes[:].rearrange("p g j -> p (g j)"),
+                    x_scales[:].rearrange("p g j -> p (g j)"),
+                    x_grouped[:].rearrange("p g j t -> p (g j t)"),
+                )
+
+        def quantize_pass(mat, e, g):
+            grouped = work.tile([P, PACK * H], BF16, name="grouped", tag="grouped", bufs=GROUPED_BUFFERS, align_bytes=64)
+            rows = landed[(mat, e, g)]
+            if mat == "w2":
+                dst = grouped[:].rearrange("p (m l u) -> p m u l", l=LINE, u=PACK)
+                src = rows[:].rearrange("p u (m l) -> p m u l", l=LINE)
+            else:
+                dst = grouped[:].rearrange("p (u m t) -> p m t u", u=PACK, t=PACK)
+                src = rows[:].rearrange("p t (m u) -> p m t u", u=PACK)
+            vector_groups = VECTOR_GROUPS[(mat, e)]
+            if vector_groups > 0:
+                nc.vector.tensor_copy(out=dst[:, :vector_groups], in_=src[:, :vector_groups])
+            nc.scalar.copy(out=dst[:, vector_groups:], in_=src[:, vector_groups:])
+            quantize(w_codes[(mat, e)][:, g, :], w_scales[(mat, e)][:, g, :], grouped[:])
+
+        def first_layer_group(bank_slice, mat, e, u, cols):
+            for g in range(PASSES):
+                nc.tensor.matmul_mx(
+                    out=bank_slice,
+                    lhsT=w_codes[(mat, e)][:, g, u * P:(u + 1) * P].bitcast(FP8X4),
+                    lhsT_scale=w_scales[(mat, e)][:, g, u * P:(u + 1) * P],
+                    rhs=x_codes[:, g, cols].bitcast(FP8X4),
+                    rhs_scale=x_scales[:, g, cols],
+                    start=(g == 0),
+                    stop=(g == PASSES - 1),
+                )
+
+        def w3_sums(e):
+            for c in range(CHUNKS):
+                w3_banks[(e, c)] = psum.tile([P, PACK, CHUNK], F32, name="bank_w3", tag="bank_w3")
+                for u in range(PACK):
+                    first_layer_group(w3_banks[(e, c)][:, u, :], "w3", e, u, slice(e * C + c * CHUNK, e * C + (c + 1) * CHUNK))
+
+        def w1_sums(e):
+            gelu_tiles[e] = work.tile([P, PACK, C], F32, name="gelu_a", tag="gelu_a")
+            for u0 in range(0, PACK, 2):
+                bank = psum.tile([P, 2, C], F32, name="bank_w1", tag="bank_w1")
+                for q in range(2):
+                    first_layer_group(bank[:, q, :], "w1", e, u0 + q, slice(e * C, (e + 1) * C))
+                nc.scalar.activation(out=gelu_tiles[e][:, u0:u0 + 2, :], in_=bank[:], func=GELU)
+
+        def hidden(e):
+            h_grouped = work.tile([P, C, PACK], BF16, name="h_grouped", tag="h_grouped", align_bytes=64)
+            for c in range(CHUNKS):
+                nc.vector.tensor_tensor(
+                    out=h_grouped[:, c * CHUNK:(c + 1) * CHUNK, :],
+                    in0=w3_banks[(e, c)][:].rearrange("p u j -> p j u"),
+                    in1=gelu_tiles[e][:, :, c * CHUNK:(c + 1) * CHUNK].rearrange("p u j -> p j u"),
+                    op=MULT,
+                )
+            quantize(h_codes[e][:], h_scales[e][:], h_grouped[:].rearrange("p j u -> p (j u)"))
+
+        def second_layer(e, pair):
+            bank = psum.tile([P, 2, C], F32, name="bank_y", tag="bank_y")
+            y_tiles[(e, pair)] = work.tile([P, 2, C], F32, name="y_sb", tag="y_sb", bufs=Y_BUFFERS)
+            for q in range(2):
+                b = 2 * pair + q
+                nc.tensor.matmul_mx(
+                    out=bank[:, q, :],
+                    lhsT=w_codes[("w2", e)][:, 0, b * P:(b + 1) * P].bitcast(FP8X4),
+                    lhsT_scale=w_scales[("w2", e)][:, 0, b * P:(b + 1) * P],
+                    rhs=h_codes[e][:].bitcast(FP8X4),
+                    rhs_scale=h_scales[e][:],
+                    start=True,
+                    stop=True,
+                )
+            if (e, pair) == (E - 1, 0):
+                for q in range(2):
+                    nc.scalar.copy(out=y_tiles[(e, pair)][:, q, :], in_=bank[:, q, :])
+            else:
+                nc.scalar.copy(out=y_tiles[(e, pair)][:], in_=bank[:])
+
+        def scatter_what_can_go():
+            for b in range(BLOCKS):
+                while turn[b] < E and (SCATTER_TURNS[b][turn[b]], b // 2) in y_tiles:
+                    e = SCATTER_TURNS[b][turn[b]]
+                    nc.vector.tensor_tensor(
+                        out=windows[b][:].indirect(offsets[:, e * LIST_COLS:(e + 1) * LIST_COLS]),
+                        in0=y_tiles[(e, b // 2)][:, b % 2, :],
+                        in1=gate_sb[(e, b // 2)][:, b % 2, :],
+                        op=MULT,
+                    )
+                    turn[b] += 1
+                    if turn[b] == E:
+                        nc.sync.dma_start(out[b * P:(b + 1) * P, :], windows[b][:])
+
+        all_planes = tuple(("x", g, t) for g in range(PASSES) for t in range(PACK))
+        stages = []
+        for e in range(E):
+            for mat in ("w3", "w1"):
+                stages.append((("sums", mat, e), all_planes + tuple((mat, e, g) for g in range(PASSES))))
+            stages.append((("hidden", e), (("sums", "w3", e), ("sums", "w1", e))))
+            for pair in range(PAIRS):
+                stages.append((("second", e, pair), (("hidden", e), ("w2", e, 0), ("gate", e, pair))))
+
+        for item in LOADS[:LOADS_AHEAD]:
+            load(item)
+        for done, item in enumerate(LOADS):
+            if done + LOADS_AHEAD < len(LOADS):
+                load(LOADS[done + LOADS_AHEAD])
+            if item[0] == "x":
+                gather_plane(item[1], item[2])
+            elif item[0] != "gate":
+                quantize_pass(item[0], item[1], item[2])
+            written.add(item)
+            for stage, needs in stages:
+                if stage not in written and all(need in written for need in needs):
+                    if stage[:2] == ("sums", "w3"):
+                        w3_sums(stage[2])
+                    elif stage[:2] == ("sums", "w1"):
+                        w1_sums(stage[2])
+                    elif stage[0] == "hidden":
+                        hidden(stage[1])
+                    else:
+                        second_layer(stage[1], stage[2])
+                        scatter_what_can_go()
+                    written.add(stage)

@@ -90,6 +90,7 @@ def tile_routed_moe_kernel(tc, xT, w1, w3, w2, gate, offs, out):
         landed = {}
         w3_banks = {}
         gelu_tiles = {}
+        y_banks = {}
         y_tiles = {}
         turn = [0] * BLOCKS
         written = set()
@@ -154,7 +155,7 @@ def tile_routed_moe_kernel(tc, xT, w1, w3, w2, gate, offs, out):
                     first_layer_group(w3_banks[(e, c)][:, u, :], "w3", e, u, slice(e * C + c * CHUNK, e * C + (c + 1) * CHUNK))
 
         def w1_sums(e):
-            gelu_tiles[e] = work.tile([P, PACK, C], F32, name="gelu_a", tag="gelu_a")
+            gelu_tiles[e] = work.tile([P, PACK, C], F32, name="gelu_a", tag="gelu_a%d" % e, bufs=1)
             for u0 in range(0, PACK, 2):
                 bank = psum.tile([P, 2, C], F32, name="bank_w1", tag="bank_w1")
                 for q in range(2):
@@ -174,7 +175,7 @@ def tile_routed_moe_kernel(tc, xT, w1, w3, w2, gate, offs, out):
 
         def second_layer(e, pair):
             bank = psum.tile([P, 2, C], F32, name="bank_y", tag="bank_y")
-            y_tiles[(e, pair)] = work.tile([P, 2, C], F32, name="y_sb", tag="y_sb", bufs=Y_BUFFERS)
+            y_banks[(e, pair)] = bank
             for q in range(2):
                 b = 2 * pair + q
                 nc.tensor.matmul_mx(
@@ -186,7 +187,14 @@ def tile_routed_moe_kernel(tc, xT, w1, w3, w2, gate, offs, out):
                     start=True,
                     stop=True,
                 )
-            if (e, pair) == (E - 1, 0):
+
+        def copy_out(e, pair):
+            bank = y_banks[(e, pair)]
+            if (e, pair) == (0, PAIRS - 1):
+                y_tiles[(e, pair)] = work.tile([P, 2, C], F32, name="y_late", tag="gelu_a%d" % (E - 1), bufs=1)
+            else:
+                y_tiles[(e, pair)] = work.tile([P, 2, C], F32, name="y_sb", tag="y_sb", bufs=Y_BUFFERS)
+            if (e, pair) in ((E - 1, 0), (0, PAIRS - 1)):
                 for q in range(2):
                     nc.scalar.copy(out=y_tiles[(e, pair)][:, q, :], in_=bank[:, q, :])
             else:
@@ -194,7 +202,7 @@ def tile_routed_moe_kernel(tc, xT, w1, w3, w2, gate, offs, out):
 
         def scatter_what_can_go():
             for b in range(BLOCKS):
-                while turn[b] < E and (SCATTER_TURNS[b][turn[b]], b // 2) in y_tiles:
+                while turn[b] < E and (SCATTER_TURNS[b][turn[b]], b // 2) in y_tiles and ("gate", SCATTER_TURNS[b][turn[b]], b // 2) in written:
                     e = SCATTER_TURNS[b][turn[b]]
                     nc.vector.tensor_tensor(
                         out=windows[b][:].indirect(offsets[:, e * LIST_COLS:(e + 1) * LIST_COLS]),
@@ -213,7 +221,8 @@ def tile_routed_moe_kernel(tc, xT, w1, w3, w2, gate, offs, out):
                 stages.append((("sums", mat, e), all_planes + tuple((mat, e, g) for g in range(PASSES))))
             stages.append((("hidden", e), (("sums", "w3", e), ("sums", "w1", e))))
             for pair in range(PAIRS):
-                stages.append((("second", e, pair), (("hidden", e), ("w2", e, 0), ("gate", e, pair))))
+                stages.append((("second", e, pair), (("hidden", e), ("w2", e, 0))))
+                stages.append((("copy", e, pair), (("second", e, pair),) + ((("hidden", E - 1),) if (e, pair) == (0, PAIRS - 1) else ())))
 
         for item in LOADS[:LOADS_AHEAD]:
             load(item)
@@ -233,7 +242,9 @@ def tile_routed_moe_kernel(tc, xT, w1, w3, w2, gate, offs, out):
                         w1_sums(stage[2])
                     elif stage[0] == "hidden":
                         hidden(stage[1])
-                    else:
+                    elif stage[0] == "second":
                         second_layer(stage[1], stage[2])
-                        scatter_what_can_go()
+                    else:
+                        copy_out(stage[1], stage[2])
                     written.add(stage)
+            scatter_what_can_go()

@@ -30,14 +30,16 @@ LOADS = (
     tuple(("x", g, t) for g in range(PASSES) for t in range(PACK))
     + tuple((mat, 0, g) for mat in ("w3", "w1") for g in range(PASSES))
     + (("w3", 1, 0), ("w3", 1, 1), ("w1", 1, 0), ("w2", 0, 0), ("w1", 1, 1))
-    + (("gate", 0, 0), ("w2", 1, 0), ("gate", 1, 0), ("gate", 0, 1), ("gate", 1, 1))
+    + (("gate", 1, 0), ("gate", 0, 1), ("gate", 0, 0), ("w2", 1, 0), ("gate", 1, 1))
 )
 LOADS_AHEAD = 4
 LOAD_BUFFERS = 6
 GROUPED_BUFFERS = 4
 Y_BUFFERS = 3
 
-VECTOR_GROUPS = {("w3", 0): 64, ("w1", 0): 64, ("w3", 1): 64, ("w1", 1): 64, ("w2", 0): 48, ("w2", 1): 0}
+VECTOR_GROUPS = {("w3", 0, 0): 64, ("w3", 0, 1): 64, ("w1", 0, 0): 64, ("w1", 0, 1): 64, ("w3", 1, 0): 64, ("w3", 1, 1): 64, ("w1", 1, 0): 64, ("w1", 1, 1): 64, ("w2", 0, 0): 48, ("w2", 1, 0): 0}
+TIES = {0: None, 1: None, 2: ("p", 1), 3: None}
+SPLIT_PASSES = (("w1", 1, 1),)
 
 SCATTER_TURNS = ((0, 1), (0, 1), (0, 1), (1, 0))
 
@@ -92,6 +94,7 @@ def tile_routed_moe_kernel(tc, xT, w1, w3, w2, gate, offs, out):
         gelu_tiles = {}
         y_banks = {}
         y_tiles = {}
+        y0_tiles = {}
         turn = [0] * BLOCKS
         written = set()
 
@@ -105,8 +108,13 @@ def tile_routed_moe_kernel(tc, xT, w1, w3, w2, gate, offs, out):
                 nc.sync.dma_start(landed[item][:], x_planes[g, :, t, :])
             else:
                 mat, e, g = item
-                landed[item] = ring.tile([P, PACK, H], F32, name="rows", tag="landed")
-                nc.sync.dma_start(landed[item][:], w_passes[mat][e, g])
+                if item in SPLIT_PASSES:
+                    for half in range(2):
+                        landed[(item, half)] = ring.tile([P, 2, H], F32, name="row_pair", tag="landed")
+                        nc.sync.dma_start(landed[(item, half)][:], w_passes[mat][e, g][:, 2 * half:2 * half + 2, :])
+                else:
+                    landed[item] = ring.tile([P, PACK, H], F32, name="rows", tag="landed")
+                    nc.sync.dma_start(landed[item][:], w_passes[mat][e, g])
 
         def quantize(codes, scales, grouped):
             nc.vector.quantize_mx(out=codes.bitcast(FP8X4), scales=scales, in_=grouped)
@@ -122,7 +130,16 @@ def tile_routed_moe_kernel(tc, xT, w1, w3, w2, gate, offs, out):
                 )
 
         def quantize_pass(mat, e, g):
-            grouped = work.tile([P, PACK * H], BF16, name="grouped", tag="grouped", bufs=GROUPED_BUFFERS, align_bytes=64)
+            if ("q", mat, e, g) in TIES.values():
+                grouped = work.tile([P, PACK * H], BF16, name="grouped_t", tag="grouped_%s%d%d" % (mat, e, g), bufs=1, align_bytes=64)
+            else:
+                grouped = work.tile([P, PACK * H], BF16, name="grouped", tag="grouped", bufs=GROUPED_BUFFERS, align_bytes=64)
+            if (mat, e, g) in SPLIT_PASSES:
+                dst = grouped[:].rearrange("p (u m t) -> p m t u", u=PACK, t=PACK)
+                nc.scalar.copy(out=dst[:, :, 0:2, :], in_=landed[((mat, e, g), 0)][:].rearrange("p t (m u) -> p m t u", u=PACK))
+                nc.vector.tensor_copy(out=dst[:, :, 2:4, :], in_=landed[((mat, e, g), 1)][:].rearrange("p t (m u) -> p m t u", u=PACK))
+                quantize(w_codes[(mat, e)][:, g, :], w_scales[(mat, e)][:, g, :], grouped[:])
+                return
             rows = landed[(mat, e, g)]
             if mat == "w2":
                 dst = grouped[:].rearrange("p (m l u) -> p m u l", l=LINE, u=PACK)
@@ -130,10 +147,11 @@ def tile_routed_moe_kernel(tc, xT, w1, w3, w2, gate, offs, out):
             else:
                 dst = grouped[:].rearrange("p (u m t) -> p m t u", u=PACK, t=PACK)
                 src = rows[:].rearrange("p t (m u) -> p m t u", u=PACK)
-            vector_groups = VECTOR_GROUPS[(mat, e)]
+            vector_groups = VECTOR_GROUPS[(mat, e, g)]
             if vector_groups > 0:
                 nc.vector.tensor_copy(out=dst[:, :vector_groups], in_=src[:, :vector_groups])
-            nc.scalar.copy(out=dst[:, vector_groups:], in_=src[:, vector_groups:])
+            if vector_groups < P:
+                nc.scalar.copy(out=dst[:, vector_groups:], in_=src[:, vector_groups:])
             quantize(w_codes[(mat, e)][:, g, :], w_scales[(mat, e)][:, g, :], grouped[:])
 
         def first_layer_group(bank_slice, mat, e, u, cols):
@@ -163,7 +181,7 @@ def tile_routed_moe_kernel(tc, xT, w1, w3, w2, gate, offs, out):
                 nc.scalar.activation(out=gelu_tiles[e][:, u0:u0 + 2, :], in_=bank[:], func=GELU)
 
         def hidden(e):
-            h_grouped = work.tile([P, C, PACK], BF16, name="h_grouped", tag="h_grouped", align_bytes=64)
+            h_grouped = work.tile([P, C, PACK], BF16, name="h_grouped", tag="h_grouped%d" % e, bufs=1, align_bytes=64)
             for c in range(CHUNKS):
                 nc.vector.tensor_tensor(
                     out=h_grouped[:, c * CHUNK:(c + 1) * CHUNK, :],
@@ -188,13 +206,22 @@ def tile_routed_moe_kernel(tc, xT, w1, w3, w2, gate, offs, out):
                     stop=True,
                 )
 
+        def copy_block(b):
+            tie = TIES[b]
+            if tie is None:
+                y0_tiles[b] = work.tile([P, C], F32, name="y0", tag="y0_%d" % b, bufs=1, align_bytes=64)
+            elif tie[0] == "q":
+                y0_tiles[b] = work.tile([P, C], F32, name="y0", tag="grouped_%s%d%d" % tie[1:], bufs=1, align_bytes=64)
+            elif tie[0] == "p":
+                y0_tiles[b] = work.tile([P, C], F32, name="y0", tag="gelu_a%d" % tie[1], bufs=1)
+            else:
+                y0_tiles[b] = work.tile([P, C], F32, name="y0", tag="h_grouped%d" % tie[1], bufs=1, align_bytes=64)
+            nc.scalar.copy(out=y0_tiles[b][:], in_=y_banks[(0, b // 2)][:, b % 2, :])
+
         def copy_out(e, pair):
             bank = y_banks[(e, pair)]
-            if (e, pair) == (0, PAIRS - 1):
-                y_tiles[(e, pair)] = work.tile([P, 2, C], F32, name="y_late", tag="gelu_a%d" % (E - 1), bufs=1)
-            else:
-                y_tiles[(e, pair)] = work.tile([P, 2, C], F32, name="y_sb", tag="y_sb", bufs=Y_BUFFERS)
-            if (e, pair) in ((E - 1, 0), (0, PAIRS - 1)):
+            y_tiles[(e, pair)] = work.tile([P, 2, C], F32, name="y_sb", tag="y_sb", bufs=Y_BUFFERS)
+            if (e, pair) == (E - 1, 0):
                 for q in range(2):
                     nc.scalar.copy(out=y_tiles[(e, pair)][:, q, :], in_=bank[:, q, :])
             else:
@@ -202,11 +229,11 @@ def tile_routed_moe_kernel(tc, xT, w1, w3, w2, gate, offs, out):
 
         def scatter_what_can_go():
             for b in range(BLOCKS):
-                while turn[b] < E and (SCATTER_TURNS[b][turn[b]], b // 2) in y_tiles and ("gate", SCATTER_TURNS[b][turn[b]], b // 2) in written:
+                while turn[b] < E and ((SCATTER_TURNS[b][turn[b]], b // 2) in y_tiles or (SCATTER_TURNS[b][turn[b]] == 0 and b in y0_tiles)) and ("gate", SCATTER_TURNS[b][turn[b]], b // 2) in written:
                     e = SCATTER_TURNS[b][turn[b]]
                     nc.vector.tensor_tensor(
                         out=windows[b][:].indirect(offsets[:, e * LIST_COLS:(e + 1) * LIST_COLS]),
-                        in0=y_tiles[(e, b // 2)][:, b % 2, :],
+                        in0=y0_tiles[b][:] if e == 0 else y_tiles[(e, b // 2)][:, b % 2, :],
                         in1=gate_sb[(e, b // 2)][:, b % 2, :],
                         op=MULT,
                     )
@@ -222,7 +249,11 @@ def tile_routed_moe_kernel(tc, xT, w1, w3, w2, gate, offs, out):
             stages.append((("hidden", e), (("sums", "w3", e), ("sums", "w1", e))))
             for pair in range(PAIRS):
                 stages.append((("second", e, pair), (("hidden", e), ("w2", e, 0))))
-                stages.append((("copy", e, pair), (("second", e, pair),) + ((("hidden", E - 1),) if (e, pair) == (0, PAIRS - 1) else ())))
+                if e > 0:
+                    stages.append((("copy", e, pair), (("second", e, pair),)))
+        for b in range(BLOCKS):
+            tie = TIES[b]
+            stages.append((("copy0", b), (("second", 0, b // 2),) + (() if tie is None else ((tie[1:],) if tie[0] == "q" else (("hidden", tie[1]),)))))
 
         for item in LOADS[:LOADS_AHEAD]:
             load(item)
@@ -244,6 +275,8 @@ def tile_routed_moe_kernel(tc, xT, w1, w3, w2, gate, offs, out):
                         hidden(stage[1])
                     elif stage[0] == "second":
                         second_layer(stage[1], stage[2])
+                    elif stage[0] == "copy0":
+                        copy_block(stage[1])
                     else:
                         copy_out(stage[1], stage[2])
                     written.add(stage)

@@ -141,6 +141,15 @@ def tile_routed_moe_kernel(tc, xT, w1, w3, w2, gate, offs, out):
                 quantize(w_codes[(mat, e)][:, g, :], w_scales[(mat, e)][:, g, :], grouped[:])
                 return
             rows = landed[(mat, e, g)]
+            if (mat, e) == ("w2", E - 1):
+                dst = grouped[:].rearrange("p (m l u) -> p m u l", l=LINE, u=PACK)
+                src = rows[:].rearrange("p u (m l) -> p m u l", l=LINE)
+                for half in range(2):
+                    groups = slice(half * P // 2, (half + 1) * P // 2)
+                    cols = slice(half * H // 2, (half + 1) * H // 2)
+                    nc.scalar.copy(out=dst[:, groups], in_=src[:, groups])
+                    quantize(w_codes[(mat, e)][:, g, cols], w_scales[(mat, e)][:, g, cols], grouped[:, half * PACK * H // 2:(half + 1) * PACK * H // 2])
+                return
             if mat == "w2":
                 dst = grouped[:].rearrange("p (m l u) -> p m u l", l=LINE, u=PACK)
                 src = rows[:].rearrange("p u (m l) -> p m u l", l=LINE)

@@ -1,11 +1,8 @@
 from contextlib import ExitStack
-
 import concourse.mybir as mybir
-
 K, T, E, C, H, N = 1024, 2048, 2, 256, 512, 512
 SLOTS = E * C
 FLOPS = 2 * SLOTS * (2 * K * H + H * N)
-
 F32 = mybir.dt.float32
 BF16 = mybir.dt.bfloat16
 U32 = mybir.dt.uint32
@@ -14,7 +11,6 @@ U8 = mybir.dt.uint8
 FP8X4 = mybir.dt.float8_e4m3fn_x4
 GELU = mybir.ActivationFunctionType.Gelu_apprx_tanh
 MULT = mybir.AluOpType.mult
-
 P = 128
 PACK = 4
 PASSES = K // (P * PACK)
@@ -24,24 +20,19 @@ BLOCKS = N // P
 PAIRS = BLOCKS // 2
 LIST_COLS = C // 16
 LINE = 4
-TABLE_COLS = 8
-
-LOADS = (
-    tuple(("x", g, t) for g in range(PASSES) for t in range(PACK))
-    + tuple((mat, 0, g) for mat in ("w3", "w1") for g in range(PASSES))
-    + (("w3", 1, 0), ("w3", 1, 1), ("w1", 1, 0), ("w2", 0, 0), ("w1", 1, 1))
-    + (("gate", 1, 0), ("gate", 0, 1), ("gate", 0, 0), ("w2", 1, 0), ("gate", 1, 1))
-)
 LOADS_AHEAD = 4
 LOAD_BUFFERS = 6
 GROUPED_BUFFERS = 4
-Y_BUFFERS = 3
-
-VECTOR_GROUPS = {("w3", 0, 0): 64, ("w3", 0, 1): 64, ("w1", 0, 0): 64, ("w1", 0, 1): 64, ("w3", 1, 0): 64, ("w3", 1, 1): 64, ("w1", 1, 0): 64, ("w1", 1, 1): 64, ("w2", 0, 0): 48, ("w2", 1, 0): 0}
-TIES = {0: None, 1: None, 2: ("p", 1), 3: None}
-SPLIT_PASSES = (("w1", 1, 1),)
-
+LOADS = (('x', 0, 0), ('x', 0, 1), ('x', 0, 2), ('x', 0, 3), ('x', 1, 0), ('x', 1, 1), ('x', 1, 2), ('x', 1, 3), ('w3', 0, 0), ('w3', 0, 1), ('w1', 0, 0), ('w1', 0, 1), ('w2h', 0, 0), ('w3', 1, 0), ('w3', 1, 1), ('w1', 1, 0), ('gate', 0, (0,)), ('w1', 1, 1), ('w2h', 0, 1), ('gate', 0, (1,)), ('w2', 1, 0), ('gate', 1, (0, 1)), ('gate', 0, (2, 3)), ('gate', 1, (2, 3)))
+VECTOR_GROUPS = {('w3', 0, 0): 64, ('w3', 0, 1): 64, ('w1', 0, 0): 64, ('w1', 0, 1): 64, ('w3', 1, 0): 48, ('w3', 1, 1): 48, ('w1', 1, 0): 48, ('w1', 1, 1): 64, ('w2', 0, 0): 48, ('w2', 1, 0): 0, ('half', 'w1', 1, 1, 0): 0, ('half', 'w1', 1, 1, 1): 128, ('half', 'w1', 0, 1, 0): 0, ('half', 'w1', 0, 1, 1): 128, ('w2h', 0, 0): 0, ('w2h', 0, 1): 0, ('w2h', 1, 0): 0, ('w2h', 1, 1): 0}
+W2_CUTS = (1, 2)
+BANKS = (2, 4)
+W1_BUFS = 4
+TIES = {(0, 1): ('q', 'w1', 1, 1), (0, 2): ('p', 1), (0, 3): ('h', 1)}
+SCATTER_TEXT = (0, 1, 2, 3)
 SCATTER_TURNS = ((0, 1), (0, 1), (0, 1), (1, 0))
+Y_COPIES = ((0, (0,)), (0, (1,)), (0, (2,)), (0, (3,)), (1, (0,)), (1, (1,)), (1, (2, 3)))
+PRE = {}
 
 
 def tile_routed_moe_kernel(tc, xT, w1, w3, w2, gate, offs, out):
@@ -51,19 +42,15 @@ def tile_routed_moe_kernel(tc, xT, w1, w3, w2, gate, offs, out):
         ring = ctx.enter_context(tc.tile_pool(name="ring", bufs=LOAD_BUFFERS))
         work = ctx.enter_context(tc.tile_pool(name="work", bufs=E))
         psum = ctx.enter_context(tc.psum_pool(name="psum", bufs=2))
-
         offsets = held.tile([P, SLOTS // 16], U16, name="offsets")
         nc.sync.dma_start(offsets[:], offs)
-
-        table_in = held.tile([P, TABLE_COLS], F32, name="table_in")
-        table_out = held.tile([P, TABLE_COLS], F32, name="table_out")
+        table_in = held.tile([P, 8], F32, name="table_in")
+        table_out = held.tile([P, 8], F32, name="table_out")
         nc.vector.memset(table_in[:], 0.0)
         nc.scalar.activation(out=table_out[:], in_=table_in[:], func=GELU)
-
         windows = [held.tile([P, T], F32, name="window%d" % b) for b in range(BLOCKS)]
         for b in range(BLOCKS):
             nc.gpsimd.memset(windows[b][:], 0.0)
-
         picked = [held.tile([P, PACK, SLOTS], F32, name="picked%d" % g) for g in range(PASSES)]
         x_grouped = held.tile([P, PASSES, SLOTS, PACK], BF16, name="x_grouped", align_bytes=64)
         x_codes = held.tile([P, PASSES, SLOTS], U32, name="x_codes", align_bytes=64)
@@ -77,10 +64,6 @@ def tile_routed_moe_kernel(tc, xT, w1, w3, w2, gate, offs, out):
         h_codes = [held.tile([P, C], U32, name="h_codes%d" % e, align_bytes=64) for e in range(E)]
         h_scales = [held.tile([P, C], U8, name="h_scales%d" % e, align_bytes=64) for e in range(E)]
         gate_sb = {}
-        for e in range(E):
-            for pair in range(PAIRS):
-                gate_sb[(e, pair)] = held.tile([P, 2, C], F32, name="gate_sb%d%d" % (e, pair))
-
         x_planes = xT.rearrange("(g p t) v -> g p t v", p=P, t=PACK)
         w_passes = {
             "w1": w1.rearrange("e (g p t) i -> e g p t i", p=P, t=PACK),
@@ -88,36 +71,47 @@ def tile_routed_moe_kernel(tc, xT, w1, w3, w2, gate, offs, out):
             "w2": w2.rearrange("e (g p u) n -> e g p u n", p=P, u=PACK),
         }
         gate_blocks = gate.rearrange("(b p) j -> p b j", p=P)
-
         landed = {}
-        w3_banks = {}
+        banks3 = {}
+        banks1 = {}
         gelu_tiles = {}
         y_banks = {}
         y_tiles = {}
-        y0_tiles = {}
         turn = [0] * BLOCKS
         written = set()
 
         def load(item):
             if item[0] == "gate":
-                e, pair = item[1:]
-                nc.sync.dma_start(gate_sb[(e, pair)][:], gate_blocks[:, 2 * pair:2 * pair + 2, e * C:(e + 1) * C])
+                e, bs = item[1:]
+                t = held.tile([P, len(bs), C], F32, name="gate_sb%d_%d" % (e, bs[0]))
+                for i, b in enumerate(bs):
+                    gate_sb[(e, b)] = t[:, i, :]
+                nc.sync.dma_start(t[:], gate_blocks[:, bs[0]:bs[-1] + 1, e * C:(e + 1) * C])
             elif item[0] == "x":
                 g, t = item[1:]
                 landed[item] = ring.tile([P, T], F32, name="plane", tag="landed")
                 nc.sync.dma_start(landed[item][:], x_planes[g, :, t, :])
+            elif item[0] == "w2h":
+                e, half = item[1:]
+                landed[item] = ring.tile([P, PACK, H // 2], F32, name="rows", tag="landed")
+                nc.sync.dma_start(landed[item][:], w_passes["w2"][e, 0][:, :, half * (H // 2):(half + 1) * (H // 2)])
+            elif item[0] == "half":
+                mat, e, g, half = item[1:]
+                landed[item] = ring.tile([P, 2, H], F32, name="row_pair", tag="landed")
+                nc.sync.dma_start(landed[item][:], w_passes[mat][e, g][:, 2 * half:2 * half + 2, :])
             else:
                 mat, e, g = item
-                if item in SPLIT_PASSES:
-                    for half in range(2):
-                        landed[(item, half)] = ring.tile([P, 2, H], F32, name="row_pair", tag="landed")
-                        nc.sync.dma_start(landed[(item, half)][:], w_passes[mat][e, g][:, 2 * half:2 * half + 2, :])
-                else:
-                    landed[item] = ring.tile([P, PACK, H], F32, name="rows", tag="landed")
-                    nc.sync.dma_start(landed[item][:], w_passes[mat][e, g])
+                landed[item] = ring.tile([P, PACK, H], F32, name="rows", tag="landed")
+                nc.sync.dma_start(landed[item][:], w_passes[mat][e, g])
 
         def quantize(codes, scales, grouped):
             nc.vector.quantize_mx(out=codes.bitcast(FP8X4), scales=scales, in_=grouped)
+
+        def shared(dst, src, v, lo=0, hi=P):
+            if v > 0:
+                nc.vector.tensor_copy(out=dst[:, lo:lo + v], in_=src[:, lo:lo + v])
+            if lo + v < hi:
+                nc.scalar.copy(out=dst[:, lo + v:hi], in_=src[:, lo + v:hi])
 
         def gather_plane(g, t):
             nc.vector.tensor_copy(picked[g][:, t, :], landed[("x", g, t)][:].indirect(offsets[:]))
@@ -129,72 +123,102 @@ def tile_routed_moe_kernel(tc, xT, w1, w3, w2, gate, offs, out):
                     x_grouped[:].rearrange("p g j t -> p (g j t)"),
                 )
 
-        def quantize_pass(mat, e, g):
-            if ("q", mat, e, g) in TIES.values():
-                grouped = work.tile([P, PACK * H], BF16, name="grouped_t", tag="grouped_%s%d%d" % (mat, e, g), bufs=1, align_bytes=64)
-            else:
-                grouped = work.tile([P, PACK * H], BF16, name="grouped", tag="grouped", bufs=GROUPED_BUFFERS, align_bytes=64)
-            if (mat, e, g) in SPLIT_PASSES:
+        def new_grouped(key, cols):
+            if key in PRE:
+                e, b = PRE[key]
+                return work.tile([P, cols], BF16, name="grouped_y", tag="y%d_%d" % (e, b), bufs=1, align_bytes=64)
+            if key in TIES.values():
+                return work.tile([P, cols], BF16, name="grouped_t", tag="grouped_%s%d%d" % key[1:], bufs=1, align_bytes=64)
+            return work.tile([P, PACK * H], BF16, name="grouped", tag="grouped", bufs=GROUPED_BUFFERS, align_bytes=64)
+
+        grouped_halves = {}
+
+        def work_on(item):
+            if item[0] == "half":
+                mat, e, g, half = item[1:]
+                if half == 0:
+                    grouped_halves[(mat, e, g)] = new_grouped(("q", mat, e, g), PACK * H)
+                grouped = grouped_halves[(mat, e, g)]
                 dst = grouped[:].rearrange("p (u m t) -> p m t u", u=PACK, t=PACK)
-                nc.scalar.copy(out=dst[:, :, 0:2, :], in_=landed[((mat, e, g), 0)][:].rearrange("p t (m u) -> p m t u", u=PACK))
-                nc.vector.tensor_copy(out=dst[:, :, 2:4, :], in_=landed[((mat, e, g), 1)][:].rearrange("p t (m u) -> p m t u", u=PACK))
-                quantize(w_codes[(mat, e)][:, g, :], w_scales[(mat, e)][:, g, :], grouped[:])
+                shared(dst[:, :, 2 * half:2 * half + 2, :], landed[item][:].rearrange("p t (m u) -> p m t u", u=PACK), VECTOR_GROUPS[item])
+                if half == 1:
+                    quantize(w_codes[(mat, e)][:, g, :], w_scales[(mat, e)][:, g, :], grouped[:])
+                    written.add((mat, e, g))
                 return
-            rows = landed[(mat, e, g)]
-            if (mat, e) == ("w2", E - 1):
-                dst = grouped[:].rearrange("p (m l u) -> p m u l", l=LINE, u=PACK)
-                src = rows[:].rearrange("p u (m l) -> p m u l", l=LINE)
-                for half in range(2):
-                    groups = slice(half * P // 2, (half + 1) * P // 2)
-                    cols = slice(half * H // 2, (half + 1) * H // 2)
-                    nc.scalar.copy(out=dst[:, groups], in_=src[:, groups])
-                    quantize(w_codes[(mat, e)][:, g, cols], w_scales[(mat, e)][:, g, cols], grouped[:, half * PACK * H // 2:(half + 1) * PACK * H // 2])
+            if item[0] == "w2h":
+                e, half = item[1:]
+                grouped = new_grouped(("q", "w2", e, half), PACK * H // 2)
+                g2 = grouped[:, 0:PACK * H // 2]
+                dst = g2.rearrange("p (m l u) -> p m u l", l=LINE, u=PACK)
+                src = landed[item][:].rearrange("p u (m l) -> p m u l", l=LINE)
+                shared(dst, src, VECTOR_GROUPS[item], 0, P // 2)
+                cols = slice(half * H // 2, (half + 1) * H // 2)
+                quantize(w_codes[("w2", e)][:, 0, cols], w_scales[("w2", e)][:, 0, cols], g2)
                 return
+            mat, e, g = item
+            grouped = new_grouped(("q", mat, e, g), PACK * H)
+            rows = landed[item]
             if mat == "w2":
                 dst = grouped[:].rearrange("p (m l u) -> p m u l", l=LINE, u=PACK)
                 src = rows[:].rearrange("p u (m l) -> p m u l", l=LINE)
-            else:
-                dst = grouped[:].rearrange("p (u m t) -> p m t u", u=PACK, t=PACK)
-                src = rows[:].rearrange("p t (m u) -> p m t u", u=PACK)
-            vector_groups = VECTOR_GROUPS[(mat, e, g)]
-            if vector_groups > 0:
-                nc.vector.tensor_copy(out=dst[:, :vector_groups], in_=src[:, :vector_groups])
-            if vector_groups < P:
-                nc.scalar.copy(out=dst[:, vector_groups:], in_=src[:, vector_groups:])
+                cuts = W2_CUTS[e]
+                for half in range(cuts):
+                    shared(dst, src, VECTOR_GROUPS[item] // cuts, half * P // cuts, (half + 1) * P // cuts)
+                    cols = slice(half * H // cuts, (half + 1) * H // cuts)
+                    quantize(w_codes[(mat, e)][:, g, cols], w_scales[(mat, e)][:, g, cols], grouped[:, half * PACK * H // cuts:(half + 1) * PACK * H // cuts])
+                written.add(("w2h", e, 0))
+                written.add(("w2h", e, 1))
+                return
+            dst = grouped[:].rearrange("p (u m t) -> p m t u", u=PACK, t=PACK)
+            src = rows[:].rearrange("p t (m u) -> p m t u", u=PACK)
+            shared(dst, src, VECTOR_GROUPS[item])
             quantize(w_codes[(mat, e)][:, g, :], w_scales[(mat, e)][:, g, :], grouped[:])
 
-        def first_layer_group(bank_slice, mat, e, u, cols):
-            for g in range(PASSES):
-                nc.tensor.matmul_mx(
-                    out=bank_slice,
-                    lhsT=w_codes[(mat, e)][:, g, u * P:(u + 1) * P].bitcast(FP8X4),
-                    lhsT_scale=w_scales[(mat, e)][:, g, u * P:(u + 1) * P],
-                    rhs=x_codes[:, g, cols].bitcast(FP8X4),
-                    rhs_scale=x_scales[:, g, cols],
-                    start=(g == 0),
-                    stop=(g == PASSES - 1),
-                )
+        def mm1(bank_slice, mat, e, u, cols, g, start, stop):
+            nc.tensor.matmul_mx(
+                out=bank_slice,
+                lhsT=w_codes[(mat, e)][:, g, u * P:(u + 1) * P].bitcast(FP8X4),
+                lhsT_scale=w_scales[(mat, e)][:, g, u * P:(u + 1) * P],
+                rhs=x_codes[:, g, cols].bitcast(FP8X4),
+                rhs_scale=x_scales[:, g, cols],
+                start=start,
+                stop=stop,
+            )
 
         def w3_sums(e):
             for c in range(CHUNKS):
-                w3_banks[(e, c)] = psum.tile([P, PACK, CHUNK], F32, name="bank_w3", tag="bank_w3")
+                banks3[(e, c)] = psum.tile([P, PACK, CHUNK], F32, name="bank_w3", tag="bank_w3")
                 for u in range(PACK):
-                    first_layer_group(w3_banks[(e, c)][:, u, :], "w3", e, u, slice(e * C + c * CHUNK, e * C + (c + 1) * CHUNK))
+                    for g in range(PASSES):
+                        mm1(banks3[(e, c)][:, u, :], "w3", e, u, slice(e * C + c * CHUNK, e * C + (c + 1) * CHUNK), g, g == 0, g == PASSES - 1)
 
-        def w1_sums(e):
-            gelu_tiles[e] = work.tile([P, PACK, C], F32, name="gelu_a", tag="gelu_a%d" % e, bufs=1)
-            for u0 in range(0, PACK, 2):
-                bank = psum.tile([P, 2, C], F32, name="bank_w1", tag="bank_w1")
-                for q in range(2):
-                    first_layer_group(bank[:, q, :], "w1", e, u0 + q, slice(e * C, (e + 1) * C))
-                nc.scalar.activation(out=gelu_tiles[e][:, u0:u0 + 2, :], in_=bank[:], func=GELU)
+        def w1_pass(e, g):
+            if BANKS[e] == 2:
+                if g == 0:
+                    return
+                gelu_tiles[e] = work.tile([P, PACK, C], F32, name="gelu_a", tag="gelu_a%d" % e, bufs=1)
+                for u0 in range(0, PACK, 2):
+                    bank = psum.tile([P, 2, C], F32, name="bank_w1", tag="bank_w1", bufs=W1_BUFS)
+                    for q in range(2):
+                        for gg in range(PASSES):
+                            mm1(bank[:, q, :], "w1", e, u0 + q, slice(e * C, (e + 1) * C), gg, gg == 0, gg == PASSES - 1)
+                    nc.scalar.activation(out=gelu_tiles[e][:, u0:u0 + 2, :], in_=bank[:], func=GELU)
+                return
+            if g == 0:
+                banks1[e] = [psum.tile([P, C], F32, name="bank_w1o", tag="bank_w1", bufs=W1_BUFS) for u in range(PACK)]
+            else:
+                gelu_tiles[e] = work.tile([P, PACK, C], F32, name="gelu_a", tag="gelu_a%d" % e, bufs=1)
+            for u in range(PACK):
+                mm1(banks1[e][u][:], "w1", e, u, slice(e * C, (e + 1) * C), g, g == 0, g == PASSES - 1)
+                if g == PASSES - 1:
+                    nc.scalar.activation(out=gelu_tiles[e][:, u, :], in_=banks1[e][u][:], func=GELU)
 
         def hidden(e):
             h_grouped = work.tile([P, C, PACK], BF16, name="h_grouped", tag="h_grouped%d" % e, bufs=1, align_bytes=64)
             for c in range(CHUNKS):
                 nc.vector.tensor_tensor(
                     out=h_grouped[:, c * CHUNK:(c + 1) * CHUNK, :],
-                    in0=w3_banks[(e, c)][:].rearrange("p u j -> p j u"),
+                    in0=banks3[(e, c)][:].rearrange("p u j -> p j u"),
                     in1=gelu_tiles[e][:, :, c * CHUNK:(c + 1) * CHUNK].rearrange("p u j -> p j u"),
                     op=MULT,
                 )
@@ -215,78 +239,72 @@ def tile_routed_moe_kernel(tc, xT, w1, w3, w2, gate, offs, out):
                     stop=True,
                 )
 
-        def copy_block(b):
-            tie = TIES[b]
+        def y_tile(e, bs):
+            tie = TIES.get((e, bs[0]))
             if tie is None:
-                y0_tiles[b] = work.tile([P, C], F32, name="y0", tag="y0_%d" % b, bufs=1, align_bytes=64)
+                t = work.tile([P, len(bs), C], F32, name="y_sb", tag="y%d_%d" % (e, bs[0]), bufs=1, align_bytes=64)
             elif tie[0] == "q":
-                y0_tiles[b] = work.tile([P, C], F32, name="y0", tag="grouped_%s%d%d" % tie[1:], bufs=1, align_bytes=64)
+                t = work.tile([P, len(bs), C], F32, name="y_sb", tag="grouped_%s%d%d" % tie[1:], bufs=1, align_bytes=64)
             elif tie[0] == "p":
-                y0_tiles[b] = work.tile([P, C], F32, name="y0", tag="gelu_a%d" % tie[1], bufs=1)
+                t = work.tile([P, len(bs), C], F32, name="y_sb", tag="gelu_a%d" % tie[1], bufs=1)
             else:
-                y0_tiles[b] = work.tile([P, C], F32, name="y0", tag="h_grouped%d" % tie[1], bufs=1, align_bytes=64)
-            nc.scalar.copy(out=y0_tiles[b][:], in_=y_banks[(0, b // 2)][:, b % 2, :])
-
-        def copy_out(e, pair):
-            bank = y_banks[(e, pair)]
-            y_tiles[(e, pair)] = work.tile([P, 2, C], F32, name="y_sb", tag="y_sb", bufs=Y_BUFFERS)
-            if (e, pair) == (E - 1, 0):
-                for q in range(2):
-                    nc.scalar.copy(out=y_tiles[(e, pair)][:, q, :], in_=bank[:, q, :])
-            else:
-                nc.scalar.copy(out=y_tiles[(e, pair)][:], in_=bank[:])
+                t = work.tile([P, len(bs), C], F32, name="y_sb", tag="h_grouped%d" % tie[1], bufs=1, align_bytes=64)
+            nc.scalar.copy(out=t[:], in_=y_banks[(e, bs[0] // 2)][:, bs[0] % 2:bs[0] % 2 + len(bs), :])
+            for i, b in enumerate(bs):
+                y_tiles[(e, b)] = t[:, i, :]
 
         def scatter_what_can_go():
-            for b in range(BLOCKS):
-                while turn[b] < E and ((SCATTER_TURNS[b][turn[b]], b // 2) in y_tiles or (SCATTER_TURNS[b][turn[b]] == 0 and b in y0_tiles)) and ("gate", SCATTER_TURNS[b][turn[b]], b // 2) in written:
+            for b in SCATTER_TEXT:
+                while turn[b] < E and (SCATTER_TURNS[b][turn[b]], b) in y_tiles and (SCATTER_TURNS[b][turn[b]], b) in gate_sb:
                     e = SCATTER_TURNS[b][turn[b]]
                     nc.vector.tensor_tensor(
                         out=windows[b][:].indirect(offsets[:, e * LIST_COLS:(e + 1) * LIST_COLS]),
-                        in0=y0_tiles[b][:] if e == 0 else y_tiles[(e, b // 2)][:, b % 2, :],
-                        in1=gate_sb[(e, b // 2)][:, b % 2, :],
+                        in0=y_tiles[(e, b)],
+                        in1=gate_sb[(e, b)],
                         op=MULT,
                     )
                     turn[b] += 1
                     if turn[b] == E:
                         nc.sync.dma_start(out[b * P:(b + 1) * P, :], windows[b][:])
 
-        all_planes = tuple(("x", g, t) for g in range(PASSES) for t in range(PACK))
         stages = []
+        all_planes = tuple(("x", g, t) for g in range(PASSES) for t in range(PACK))
         for e in range(E):
-            for mat in ("w3", "w1"):
-                stages.append((("sums", mat, e), all_planes + tuple((mat, e, g) for g in range(PASSES))))
-            stages.append((("hidden", e), (("sums", "w3", e), ("sums", "w1", e))))
+            stages.append((("w3", "sums", e), all_planes + tuple(("w3", e, g) for g in range(PASSES))))
+            stages.append((("w1", "pass", e, 0), all_planes + (("w1", e, 0),)))
+            stages.append((("w1", "pass", e, 1), (("w1", "pass", e, 0), ("w1", e, 1))))
+            stages.append((("hidden", e), (("w3", "sums", e), ("w1", "pass", e, 1))))
             for pair in range(PAIRS):
-                stages.append((("second", e, pair), (("hidden", e), ("w2", e, 0))))
-                if e > 0:
-                    stages.append((("copy", e, pair), (("second", e, pair),)))
-        for b in range(BLOCKS):
-            tie = TIES[b]
-            stages.append((("copy0", b), (("second", 0, b // 2),) + (() if tie is None else ((tie[1:],) if tie[0] == "q" else (("hidden", tie[1]),)))))
+                stages.append((("second", e, pair), (("hidden", e), ("w2h", e, pair))))
+        for e, bs in Y_COPIES:
+            tie = TIES.get((e, bs[0]))
+            needs = (("second", e, bs[0] // 2),)
+            if tie is not None:
+                needs = needs + ((("w2h",) + tie[2:] if tie[1] == "w2" else tie[1:]) if tie[0] == "q" else ("hidden", tie[1]),)
+            stages.append((("copy", e, bs), needs))
 
         for item in LOADS[:LOADS_AHEAD]:
             load(item)
         for done, item in enumerate(LOADS):
             if done + LOADS_AHEAD < len(LOADS):
                 load(LOADS[done + LOADS_AHEAD])
+            written.add(item)
             if item[0] == "x":
                 gather_plane(item[1], item[2])
             elif item[0] != "gate":
-                quantize_pass(item[0], item[1], item[2])
-            written.add(item)
+                work_on(item)
             for stage, needs in stages:
                 if stage not in written and all(need in written for need in needs):
-                    if stage[:2] == ("sums", "w3"):
+                    if stage[1] == "sums":
                         w3_sums(stage[2])
-                    elif stage[:2] == ("sums", "w1"):
-                        w1_sums(stage[2])
+                    elif stage[1] == "pass":
+                        w1_pass(stage[2], stage[3])
                     elif stage[0] == "hidden":
                         hidden(stage[1])
                     elif stage[0] == "second":
                         second_layer(stage[1], stage[2])
-                    elif stage[0] == "copy0":
-                        copy_block(stage[1])
                     else:
-                        copy_out(stage[1], stage[2])
+                        y_tile(stage[1], stage[2])
                     written.add(stage)
             scatter_what_can_go()
+        assert turn == [E] * BLOCKS

from contextlib import ExitStack
import concourse.mybir as mybir
K, T, E, C, H, N = 1024, 2048, 2, 256, 512, 512
SLOTS = E * C
FLOPS = 2 * SLOTS * (2 * K * H + H * N)
F32 = mybir.dt.float32
BF16 = mybir.dt.bfloat16
U32 = mybir.dt.uint32
U16 = mybir.dt.uint16
U8 = mybir.dt.uint8
FP8X4 = mybir.dt.float8_e4m3fn_x4
GELU = mybir.ActivationFunctionType.Gelu_apprx_tanh
MULT = mybir.AluOpType.mult
P = 128
PACK = 4
PASSES = K // (P * PACK)
CHUNK = 128
CHUNKS = C // CHUNK
BLOCKS = N // P
PAIRS = BLOCKS // 2
LIST_COLS = C // 16
LINE = 4
LOADS_AHEAD = 4
LOAD_BUFFERS = 6
GROUPED_BUFFERS = 4
LOADS = (('x', 0, 0), ('x', 0, 1), ('x', 0, 2), ('x', 0, 3), ('x', 1, 0), ('x', 1, 1), ('x', 1, 2), ('x', 1, 3), ('w3', 0, 0), ('w3', 0, 1), ('w1', 0, 0), ('w1', 0, 1), ('w2h', 0, 0), ('w3', 1, 0), ('w3', 1, 1), ('w1', 1, 0), ('gate', 0, (0,)), ('w1', 1, 1), ('w2h', 0, 1), ('gate', 0, (1,)), ('w2', 1, 0), ('gate', 1, (0, 1)), ('gate', 0, (2, 3)), ('gate', 1, (2, 3)))
VECTOR_GROUPS = {('w3', 0, 0): 64, ('w3', 0, 1): 64, ('w1', 0, 0): 64, ('w1', 0, 1): 64, ('w3', 1, 0): 48, ('w3', 1, 1): 48, ('w1', 1, 0): 48, ('w1', 1, 1): 64, ('w2', 0, 0): 48, ('w2', 1, 0): 0, ('half', 'w1', 1, 1, 0): 0, ('half', 'w1', 1, 1, 1): 128, ('half', 'w1', 0, 1, 0): 0, ('half', 'w1', 0, 1, 1): 128, ('w2h', 0, 0): 0, ('w2h', 0, 1): 0, ('w2h', 1, 0): 0, ('w2h', 1, 1): 0}
W2_CUTS = (1, 2)
BANKS = (2, 4)
W1_BUFS = 4
TIES = {(0, 1): ('q', 'w1', 1, 1), (0, 2): ('p', 1), (0, 3): ('h', 1)}
SCATTER_TEXT = (0, 1, 2, 3)
SCATTER_TURNS = ((0, 1), (0, 1), (0, 1), (1, 0))
Y_COPIES = ((0, (0,)), (0, (1,)), (0, (2,)), (0, (3,)), (1, (0,)), (1, (1,)), (1, (2, 3)))
PRE = {}


def tile_routed_moe_kernel(tc, xT, w1, w3, w2, gate, offs, out):
    nc = tc.nc
    with ExitStack() as ctx:
        held = ctx.enter_context(tc.tile_pool(name="held", bufs=1))
        ring = ctx.enter_context(tc.tile_pool(name="ring", bufs=LOAD_BUFFERS))
        work = ctx.enter_context(tc.tile_pool(name="work", bufs=E))
        psum = ctx.enter_context(tc.psum_pool(name="psum", bufs=2))
        offsets = held.tile([P, SLOTS // 16], U16, name="offsets")
        nc.sync.dma_start(offsets[:], offs)
        table_in = held.tile([P, 8], F32, name="table_in")
        table_out = held.tile([P, 8], F32, name="table_out")
        nc.vector.memset(table_in[:], 0.0)
        nc.scalar.activation(out=table_out[:], in_=table_in[:], func=GELU)
        windows = [held.tile([P, T], F32, name="window%d" % b) for b in range(BLOCKS)]
        for b in range(BLOCKS):
            nc.gpsimd.memset(windows[b][:], 0.0)
        picked = [held.tile([P, PACK, SLOTS], F32, name="picked%d" % g) for g in range(PASSES)]
        x_grouped = held.tile([P, PASSES, SLOTS, PACK], BF16, name="x_grouped", align_bytes=64)
        x_codes = held.tile([P, PASSES, SLOTS], U32, name="x_codes", align_bytes=64)
        x_scales = held.tile([P, PASSES, SLOTS], U8, name="x_scales", align_bytes=64)
        w_codes = {}
        w_scales = {}
        for e in range(E):
            for mat, passes in (("w1", PASSES), ("w3", PASSES), ("w2", 1)):
                w_codes[(mat, e)] = held.tile([P, passes, H], U32, name="%s_codes%d" % (mat, e), align_bytes=64)
                w_scales[(mat, e)] = held.tile([P, passes, H], U8, name="%s_scales%d" % (mat, e), align_bytes=64)
        h_codes = [held.tile([P, C], U32, name="h_codes%d" % e, align_bytes=64) for e in range(E)]
        h_scales = [held.tile([P, C], U8, name="h_scales%d" % e, align_bytes=64) for e in range(E)]
        gate_sb = {}
        x_planes = xT.rearrange("(g p t) v -> g p t v", p=P, t=PACK)
        w_passes = {
            "w1": w1.rearrange("e (g p t) i -> e g p t i", p=P, t=PACK),
            "w3": w3.rearrange("e (g p t) i -> e g p t i", p=P, t=PACK),
            "w2": w2.rearrange("e (g p u) n -> e g p u n", p=P, u=PACK),
        }
        gate_blocks = gate.rearrange("(b p) j -> p b j", p=P)
        landed = {}
        banks3 = {}
        banks1 = {}
        gelu_tiles = {}
        y_banks = {}
        y_tiles = {}
        turn = [0] * BLOCKS
        written = set()

        def load(item):
            if item[0] == "gate":
                e, bs = item[1:]
                t = held.tile([P, len(bs), C], F32, name="gate_sb%d_%d" % (e, bs[0]))
                for i, b in enumerate(bs):
                    gate_sb[(e, b)] = t[:, i, :]
                nc.sync.dma_start(t[:], gate_blocks[:, bs[0]:bs[-1] + 1, e * C:(e + 1) * C])
            elif item[0] == "x":
                g, t = item[1:]
                landed[item] = ring.tile([P, T], F32, name="plane", tag="landed")
                nc.sync.dma_start(landed[item][:], x_planes[g, :, t, :])
            elif item[0] == "w2h":
                e, half = item[1:]
                landed[item] = ring.tile([P, PACK, H // 2], F32, name="rows", tag="landed")
                nc.sync.dma_start(landed[item][:], w_passes["w2"][e, 0][:, :, half * (H // 2):(half + 1) * (H // 2)])
            elif item[0] == "half":
                mat, e, g, half = item[1:]
                landed[item] = ring.tile([P, 2, H], F32, name="row_pair", tag="landed")
                nc.sync.dma_start(landed[item][:], w_passes[mat][e, g][:, 2 * half:2 * half + 2, :])
            else:
                mat, e, g = item
                landed[item] = ring.tile([P, PACK, H], F32, name="rows", tag="landed")
                nc.sync.dma_start(landed[item][:], w_passes[mat][e, g])

        def quantize(codes, scales, grouped):
            nc.vector.quantize_mx(out=codes.bitcast(FP8X4), scales=scales, in_=grouped)

        def shared(dst, src, v, lo=0, hi=P):
            if v > 0:
                nc.vector.tensor_copy(out=dst[:, lo:lo + v], in_=src[:, lo:lo + v])
            if lo + v < hi:
                nc.scalar.copy(out=dst[:, lo + v:hi], in_=src[:, lo + v:hi])

        def gather_plane(g, t):
            nc.vector.tensor_copy(picked[g][:, t, :], landed[("x", g, t)][:].indirect(offsets[:]))
            nc.scalar.copy(out=x_grouped[:, g, :, t], in_=picked[g][:, t, :])
            if (g, t) == (PASSES - 1, PACK - 1):
                quantize(
                    x_codes[:].rearrange("p g j -> p (g j)"),
                    x_scales[:].rearrange("p g j -> p (g j)"),
                    x_grouped[:].rearrange("p g j t -> p (g j t)"),
                )

        def new_grouped(key, cols):
            if key in PRE:
                e, b = PRE[key]
                return work.tile([P, cols], BF16, name="grouped_y", tag="y%d_%d" % (e, b), bufs=1, align_bytes=64)
            if key in TIES.values():
                return work.tile([P, cols], BF16, name="grouped_t", tag="grouped_%s%d%d" % key[1:], bufs=1, align_bytes=64)
            return work.tile([P, PACK * H], BF16, name="grouped", tag="grouped", bufs=GROUPED_BUFFERS, align_bytes=64)

        grouped_halves = {}

        def work_on(item):
            if item[0] == "half":
                mat, e, g, half = item[1:]
                if half == 0:
                    grouped_halves[(mat, e, g)] = new_grouped(("q", mat, e, g), PACK * H)
                grouped = grouped_halves[(mat, e, g)]
                dst = grouped[:].rearrange("p (u m t) -> p m t u", u=PACK, t=PACK)
                shared(dst[:, :, 2 * half:2 * half + 2, :], landed[item][:].rearrange("p t (m u) -> p m t u", u=PACK), VECTOR_GROUPS[item])
                if half == 1:
                    quantize(w_codes[(mat, e)][:, g, :], w_scales[(mat, e)][:, g, :], grouped[:])
                    written.add((mat, e, g))
                return
            if item[0] == "w2h":
                e, half = item[1:]
                grouped = new_grouped(("q", "w2", e, half), PACK * H // 2)
                g2 = grouped[:, 0:PACK * H // 2]
                dst = g2.rearrange("p (m l u) -> p m u l", l=LINE, u=PACK)
                src = landed[item][:].rearrange("p u (m l) -> p m u l", l=LINE)
                shared(dst, src, VECTOR_GROUPS[item], 0, P // 2)
                cols = slice(half * H // 2, (half + 1) * H // 2)
                quantize(w_codes[("w2", e)][:, 0, cols], w_scales[("w2", e)][:, 0, cols], g2)
                return
            mat, e, g = item
            grouped = new_grouped(("q", mat, e, g), PACK * H)
            rows = landed[item]
            if mat == "w2":
                dst = grouped[:].rearrange("p (m l u) -> p m u l", l=LINE, u=PACK)
                src = rows[:].rearrange("p u (m l) -> p m u l", l=LINE)
                cuts = W2_CUTS[e]
                for half in range(cuts):
                    shared(dst, src, VECTOR_GROUPS[item] // cuts, half * P // cuts, (half + 1) * P // cuts)
                    cols = slice(half * H // cuts, (half + 1) * H // cuts)
                    quantize(w_codes[(mat, e)][:, g, cols], w_scales[(mat, e)][:, g, cols], grouped[:, half * PACK * H // cuts:(half + 1) * PACK * H // cuts])
                written.add(("w2h", e, 0))
                written.add(("w2h", e, 1))
                return
            dst = grouped[:].rearrange("p (u m t) -> p m t u", u=PACK, t=PACK)
            src = rows[:].rearrange("p t (m u) -> p m t u", u=PACK)
            shared(dst, src, VECTOR_GROUPS[item])
            quantize(w_codes[(mat, e)][:, g, :], w_scales[(mat, e)][:, g, :], grouped[:])

        def mm1(bank_slice, mat, e, u, cols, g, start, stop):
            nc.tensor.matmul_mx(
                out=bank_slice,
                lhsT=w_codes[(mat, e)][:, g, u * P:(u + 1) * P].bitcast(FP8X4),
                lhsT_scale=w_scales[(mat, e)][:, g, u * P:(u + 1) * P],
                rhs=x_codes[:, g, cols].bitcast(FP8X4),
                rhs_scale=x_scales[:, g, cols],
                start=start,
                stop=stop,
            )

        def w3_sums(e):
            for c in range(CHUNKS):
                banks3[(e, c)] = psum.tile([P, PACK, CHUNK], F32, name="bank_w3", tag="bank_w3")
                for u in range(PACK):
                    for g in range(PASSES):
                        mm1(banks3[(e, c)][:, u, :], "w3", e, u, slice(e * C + c * CHUNK, e * C + (c + 1) * CHUNK), g, g == 0, g == PASSES - 1)

        def w1_pass(e, g):
            if BANKS[e] == 2:
                if g == 0:
                    return
                gelu_tiles[e] = work.tile([P, PACK, C], F32, name="gelu_a", tag="gelu_a%d" % e, bufs=1)
                for u0 in range(0, PACK, 2):
                    bank = psum.tile([P, 2, C], F32, name="bank_w1", tag="bank_w1", bufs=W1_BUFS)
                    for q in range(2):
                        for gg in range(PASSES):
                            mm1(bank[:, q, :], "w1", e, u0 + q, slice(e * C, (e + 1) * C), gg, gg == 0, gg == PASSES - 1)
                    nc.scalar.activation(out=gelu_tiles[e][:, u0:u0 + 2, :], in_=bank[:], func=GELU)
                return
            if g == 0:
                banks1[e] = [psum.tile([P, C], F32, name="bank_w1o", tag="bank_w1", bufs=W1_BUFS) for u in range(PACK)]
            else:
                gelu_tiles[e] = work.tile([P, PACK, C], F32, name="gelu_a", tag="gelu_a%d" % e, bufs=1)
            for u in range(PACK):
                mm1(banks1[e][u][:], "w1", e, u, slice(e * C, (e + 1) * C), g, g == 0, g == PASSES - 1)
                if g == PASSES - 1:
                    nc.scalar.activation(out=gelu_tiles[e][:, u, :], in_=banks1[e][u][:], func=GELU)

        def hidden(e):
            h_grouped = work.tile([P, C, PACK], BF16, name="h_grouped", tag="h_grouped%d" % e, bufs=1, align_bytes=64)
            for c in range(CHUNKS):
                nc.vector.tensor_tensor(
                    out=h_grouped[:, c * CHUNK:(c + 1) * CHUNK, :],
                    in0=banks3[(e, c)][:].rearrange("p u j -> p j u"),
                    in1=gelu_tiles[e][:, :, c * CHUNK:(c + 1) * CHUNK].rearrange("p u j -> p j u"),
                    op=MULT,
                )
            quantize(h_codes[e][:], h_scales[e][:], h_grouped[:].rearrange("p j u -> p (j u)"))

        def second_layer(e, pair):
            bank = psum.tile([P, 2, C], F32, name="bank_y", tag="bank_y")
            y_banks[(e, pair)] = bank
            for q in range(2):
                b = 2 * pair + q
                nc.tensor.matmul_mx(
                    out=bank[:, q, :],
                    lhsT=w_codes[("w2", e)][:, 0, b * P:(b + 1) * P].bitcast(FP8X4),
                    lhsT_scale=w_scales[("w2", e)][:, 0, b * P:(b + 1) * P],
                    rhs=h_codes[e][:].bitcast(FP8X4),
                    rhs_scale=h_scales[e][:],
                    start=True,
                    stop=True,
                )

        def y_tile(e, bs):
            tie = TIES.get((e, bs[0]))
            if tie is None:
                t = work.tile([P, len(bs), C], F32, name="y_sb", tag="y%d_%d" % (e, bs[0]), bufs=1, align_bytes=64)
            elif tie[0] == "q":
                t = work.tile([P, len(bs), C], F32, name="y_sb", tag="grouped_%s%d%d" % tie[1:], bufs=1, align_bytes=64)
            elif tie[0] == "p":
                t = work.tile([P, len(bs), C], F32, name="y_sb", tag="gelu_a%d" % tie[1], bufs=1)
            else:
                t = work.tile([P, len(bs), C], F32, name="y_sb", tag="h_grouped%d" % tie[1], bufs=1, align_bytes=64)
            nc.scalar.copy(out=t[:], in_=y_banks[(e, bs[0] // 2)][:, bs[0] % 2:bs[0] % 2 + len(bs), :])
            for i, b in enumerate(bs):
                y_tiles[(e, b)] = t[:, i, :]

        def scatter_what_can_go():
            for b in SCATTER_TEXT:
                while turn[b] < E and (SCATTER_TURNS[b][turn[b]], b) in y_tiles and (SCATTER_TURNS[b][turn[b]], b) in gate_sb:
                    e = SCATTER_TURNS[b][turn[b]]
                    nc.vector.tensor_tensor(
                        out=windows[b][:].indirect(offsets[:, e * LIST_COLS:(e + 1) * LIST_COLS]),
                        in0=y_tiles[(e, b)],
                        in1=gate_sb[(e, b)],
                        op=MULT,
                    )
                    turn[b] += 1
                    if turn[b] == E:
                        nc.sync.dma_start(out[b * P:(b + 1) * P, :], windows[b][:])

        stages = []
        all_planes = tuple(("x", g, t) for g in range(PASSES) for t in range(PACK))
        for e in range(E):
            stages.append((("w3", "sums", e), all_planes + tuple(("w3", e, g) for g in range(PASSES))))
            stages.append((("w1", "pass", e, 0), all_planes + (("w1", e, 0),)))
            stages.append((("w1", "pass", e, 1), (("w1", "pass", e, 0), ("w1", e, 1))))
            stages.append((("hidden", e), (("w3", "sums", e), ("w1", "pass", e, 1))))
            for pair in range(PAIRS):
                stages.append((("second", e, pair), (("hidden", e), ("w2h", e, pair))))
        for e, bs in Y_COPIES:
            tie = TIES.get((e, bs[0]))
            needs = (("second", e, bs[0] // 2),)
            if tie is not None:
                needs = needs + ((("w2h",) + tie[2:] if tie[1] == "w2" else tie[1:]) if tie[0] == "q" else ("hidden", tie[1]),)
            stages.append((("copy", e, bs), needs))

        for item in LOADS[:LOADS_AHEAD]:
            load(item)
        for done, item in enumerate(LOADS):
            if done + LOADS_AHEAD < len(LOADS):
                load(LOADS[done + LOADS_AHEAD])
            written.add(item)
            if item[0] == "x":
                gather_plane(item[1], item[2])
            elif item[0] != "gate":
                work_on(item)
            for stage, needs in stages:
                if stage not in written and all(need in written for need in needs):
                    if stage[1] == "sums":
                        w3_sums(stage[2])
                    elif stage[1] == "pass":
                        w1_pass(stage[2], stage[3])
                    elif stage[0] == "hidden":
                        hidden(stage[1])
                    elif stage[0] == "second":
                        second_layer(stage[1], stage[2])
                    else:
                        y_tile(stage[1], stage[2])
                    written.add(stage)
            scatter_what_can_go()
        assert turn == [E] * BLOCKS
